import numpy as np
CORES = [0,1]
N = 2
def setup_inputs(rng):
    return {"x": rng.standard_normal((N, 128, 2048), dtype=np.float32)}
def reference(x):
    s = x.sum(axis=0, dtype=np.float64).astype(x.dtype)
    b = 2048 // N
    return {"y": np.stack([s[:, r * b:(r + 1) * b] for r in range(N)])}

from concourse.mybir import AluOpType

B = 1024

SCRATCH = {
    "send": ("sbuf", [128, B], "float32"),
    "land": ("sbuf", [128, B], "float32"),
}
SEMAPHORES = ["loaded", "own", "sent", "arrived", "stored"]


def rank_program(g, core, T, topo):
    rank = T.rank_of(core)
    if rank is None:
        return
    peer_rank = 1 - rank
    peer = T.cores[peer_rank]
    rid, pid, _se = topo.addr(peer)

    g.sync.dma_start(T.send[:], T.x[:, peer_rank * B:(peer_rank + 1) * B]).then_inc(T.sem.loaded, 16)
    g.scalar.dma_start(T.y[:], T.x[:, rank * B:(rank + 1) * B]).then_inc(T.sem.own, 16)

    g.wait_ge(T.sem.loaded, 16)
    g.remote_dma(T.land[:], T.send[:], T.sem.arrived, T.sem.sent, pid, rid, topo.mask(core, peer))

    g.wait_ge(T.sem.own, 16)
    g.wait_ge(T.sem.arrived, 16)
    g.dma_start(T.y[:], T.land[:], accum_op=AluOpType.add).then_inc(T.sem.stored, 16)
    g.wait_ge(T.sem.sent, 16)
    g.wait_ge(T.sem.stored, 16)
